import numpy as np, ml_dtypes
CORES = [76,84,92,100,108,116,124]
N = 7
import mx_ref
NC, K, S = 256, 2, 1
CNT = [[0,16,144,64,8,0,24],[24,0,16,0,72,88,56],[24,72,16,0,56,16,72],[0,72,0,40,88,56,0],[144,16,72,8,16,0,0],[48,0,8,72,0,40,88],[16,80,0,72,16,56,16]]
OFF = [[sum(c[:f]) for f in range(N + 1)] for c in CNT]
BF = ml_dtypes.bfloat16
def setup_inputs(rng):
    def f(*shape):
        return mx_ref.flush((rng.standard_normal(shape, dtype=np.float32) * np.exp2(rng.integers(-2, 3, shape[:-1] + (1,)))).astype(BF))
    return {"w": f(N, 128, 512), "x": f(N, 128, 4 * NC)}
def setup_inputs_blocks(rng):
    d = setup_inputs(rng)
    for k in ("w", "x"): d[k] = mx_ref.spread(d[k], rng, 4)
    return d
def setup_inputs_wide(rng):
    d = setup_inputs(rng)
    for k in ("w", "x"): d[k] = mx_ref.flush((d[k].astype(np.float32) * np.exp2(rng.integers(-8, 9, (N, 1, 1))).astype(np.float32)).astype(BF))
    return d
def setup_inputs_zeros(rng):
    d = setup_inputs(rng); v = d["x"].reshape(N, 128, -1, 4).copy()
    v[np.broadcast_to((rng.random((N, 1, v.shape[2], 1)) < 0.33), v.shape)] = 0
    d["x"] = v.reshape(d["x"].shape)
    return d
def reference(w, x):
    y = np.zeros((N, 128, K * NC), np.float32)
    for e in range(N):
        qw = mx_ref.quantize(w[e])
        for k in range(K):
            f = (e - S * k) % N
            t = np.concatenate([x[j][:, 4 * OFF[j][f]:4 * OFF[j][f + 1]] for j in range(N)], axis=1)
            y[e][:, NC * k:NC * k + NC] = mx_ref.matmul(qw, mx_ref.quantize(t))
    return {"y": y}

@@ -1,0 +1,202 @@
+from concourse.mybir import dt, ActivationFunctionType
+
+NCOL = 256
+HALF = 128
+NBANK = 4
+KEEP = 2
+HELP = 4
+
+SCRATCH = {
+    "xt": ("sbuf", [128, 4 * NCOL], "bfloat16"),
+    "wt": ("sbuf", [128, 512], "bfloat16"),
+    "wq": ("sbuf", [128, 128], "float8_e4m3fn_x4"),
+    "ws": ("sbuf", [128, 128], "uint8"),
+    "bq": ("sbuf", [128, 3 * NCOL], "float8_e4m3fn_x4"),
+    "bs": ("sbuf", [128, 3 * NCOL], "uint8"),
+    "yo": ("sbuf", [128, 2 * NCOL], "float32"),
+    "p0": ("psum", [128, 512], "float32"),
+    "p1": ("psum", [128, 512], "float32"),
+    "p2": ("psum", [128, 512], "float32"),
+    "p3": ("psum", [128, 512], "float32"),
+}
+SEMAPHORES = ["ld1", "ld2", "ldw", "q1", "q2", "qw", "fs", "fc", "a1", "a2", "a3",
+              "m0", "m1", "m2", "m3", "cv", "cs", "st", "sent"]
+
+
+def _plan(cores, cnt, topo):
+    n = len(cores)
+    every = range(topo.CORES_PER_CHIP * topo.CHIPS)
+    win = []
+    for j in range(n):
+        p, pos = 0, {}
+        for i in range(n):
+            pos[(j + i) % n] = p
+            p += cnt[j][(j + i) % n]
+        win.append({e: (pos[(e - 1) % n], pos[(e - 1) % n] + cnt[j][(e - 1) % n] + cnt[j][e])
+                    for e in range(n) if e != j and cnt[j][(e - 1) % n] + cnt[j][e] > 0})
+
+    def wid(j, e):
+        return win[j][e][1] - win[j][e][0]
+
+    via = []
+    for j in range(n):
+        me = cores[j]
+        mine = [c for c in every if topo.chip(c) == topo.chip(me) and c not in cores]
+        mine.sort(key=lambda c: topo.die(c) == topo.die(me))
+        far = sorted([e for e in win[j] if not topo.may_write(me, cores[e])], key=lambda e: -wid(j, e))
+        ports = [c for c in mine if all(topo.may_write(c, cores[e]) for e in far)]
+        v = {e: ports[i] for i, e in enumerate(far)}
+        near = sorted([e for e in win[j] if e not in v], key=lambda e: -wid(j, e))
+        free = [c for c in mine if c not in v.values()]
+        while len(near) > KEEP and len(v) < HELP:
+            v[near.pop()] = free.pop(0)
+        via.append(v)
+
+    base, groups = [], []
+    for e in range(n):
+        order = sorted([j for j in range(n) if e in win[j]], key=lambda j: (e in via[j], wid(j, e), j))
+        p, b = NCOL, {}
+        for j in order:
+            b[j] = p
+            p += wid(j, e)
+        gs, k = [], len(order)
+        while k > 0 and len(gs) < NBANK - 2:
+            i, s = k, 0
+            while i > 0 and s < HALF:
+                i -= 1
+                s += wid(order[i], e)
+            gs.insert(0, order[i:k])
+            k = i
+        if k > 0:
+            gs.insert(0, order[:k])
+        base.append(b)
+        groups.append(gs)
+    return win, via, base, groups
+
+
+def _send(g, T, topo, src, dst, plane, a, b, at, sem):
+    rid, pid, _ = topo.addr(dst)
+    m = topo.mask(src, dst)
+    if plane:
+        g.remote_dma(T.bs[:, at:at + b - a], T.bs[:, a:b], sem, T.sem.sent, pid, rid, m)
+    else:
+        g.remote_dma(T.bq[:, at:at + b - a].bitcast(dt.uint8), T.bq[:, a:b].bitcast(dt.uint8),
+                     sem, T.sem.sent, pid, rid, m)
+    return bin(m).count("1")
+
+
+def rank_program(g, core, T, topo):
+    cores, cnt = list(T.cores), T.tables["CNT"]
+    n = len(cores)
+    win, via, base, groups = _plan(cores, cnt, topo)
+    S = T.sem
+
+    def gsem(e, j):
+        for k, grp in enumerate(groups[e]):
+            if j in grp:
+                return S["a%d" % (k + 1)]
+
+    rank = T.rank_of(core)
+    if rank is None:
+        for j in range(n):
+            for e, h in via[j].items():
+                if h != core:
+                    continue
+                a, b = win[j][e]
+                fed = bin(topo.mask(cores[j], core)).count("1")
+                g.wait_ge(S.fs, fed)
+                out = _send(g, T, topo, core, cores[e], True, a, b, base[e][j], gsem(e, j))
+                g.wait_ge(S.fc, fed)
+                out += _send(g, T, topo, core, cores[e], False, a, b, base[e][j], gsem(e, j))
+                g.wait_ge(S.sent, out)
+        return
+
+    j = e = rank
+    turn = sum(cnt[j][:j])
+    for h, sem in ((0, S.ld1), (1, S.ld2)):
+        t, left, k = h * HALF, HALF, 0
+        while left > 0:
+            c = (turn + t) % NCOL
+            m = min(left, NCOL - c)
+            g.sync.dma_start(T.xt[:, 4 * t:4 * (t + m)], T.x[:, 4 * c:4 * (c + m)]).then_inc(sem, 16)
+            t, left, k = t + m, left - m, k + 1
+        g.vector.wait_ge(sem, 16 * k)
+        g.vector.quantize_mx(T.bq[:, h * HALF:(h + 1) * HALF], T.bs[:, h * HALF:(h + 1) * HALF],
+                             T.xt[:, 4 * h * HALF:4 * (h + 1) * HALF]).then_inc(S.q2 if h else S.q1, 1)
+    g.sync.dma_start(T.wt[:], T.w[:]).then_inc(S.ldw, 16)
+    g.vector.wait_ge(S.ldw, 16)
+    g.vector.quantize_mx(T.wq[:], T.ws[:], T.wt[:]).then_inc(S.qw, 1)
+
+    both = [False]
+
+    def ready(b):
+        if b > HALF and not both[0]:
+            g.wait_ge(S.q2, 1)
+            both[0] = True
+
+    def wid(d):
+        return win[j][d][1] - win[j][d][0]
+
+    sent = 0
+    g.wait_ge(S.q1, 1)
+    fed = sorted(via[j], key=lambda d: -wid(d))
+    for d in sorted(fed, key=lambda d: win[j][d][1] > HALF):
+        a, b = win[j][d]
+        ready(b)
+        sent += _send(g, T, topo, core, via[j][d], True, a, b, a, S.fs)
+    for d in fed:
+        a, b = win[j][d]
+        ready(b)
+        sent += _send(g, T, topo, core, via[j][d], False, a, b, a, S.fc)
+    for d in sorted([d for d in win[j] if d not in via[j]], key=lambda d: -wid(d)):
+        a, b = win[j][d]
+        ready(b)
+        sent += _send(g, T, topo, core, cores[d], True, a, b, base[d][j], gsem(d, j))
+        sent += _send(g, T, topo, core, cores[d], False, a, b, base[d][j], gsem(d, j))
+
+    def ycol(k, s):
+        f = (e - k) % n
+        return k * NCOL + sum(cnt[i][f] for i in range(s))
+
+    banks = [(0, NCOL, [(0, ycol(0, e), cnt[e][e]),
+                        (NCOL - cnt[e][(e - 1) % n], ycol(1, e), cnt[e][(e - 1) % n])], None, 0)]
+    for k, grp in enumerate(groups[e]):
+        hi = base[e][grp[-1]] + win[grp[-1]][e][1] - win[grp[-1]][e][0]
+        lo = min(base[e][grp[0]], hi - HALF)
+        pieces, due = [], 0
+        for s in grp:
+            c1 = cnt[s][(e - 1) % n]
+            pieces.append((base[e][s] - lo, ycol(1, s), c1))
+            pieces.append((base[e][s] + c1 - lo, ycol(0, s), cnt[s][e]))
+            due += 2 * bin(topo.mask(via[s].get(e, cores[s]), core)).count("1")
+        banks.append((lo, hi, pieces, S["a%d" % (k + 1)], due))
+
+    g.tensor.wait_ge(S.qw, 1)
+    g.tensor.wait_ge(S.q1, 1)
+    g.tensor.wait_ge(S.q2, 1)
+    done = {"cv": 0, "cs": 0}
+    for k, (lo, hi, pieces, sem, due) in enumerate(banks):
+        if sem is not None:
+            g.tensor.wait_ge(sem, due)
+        ps = T["p%d" % k]
+        g.tensor.matmul_mx(ps[:, 0:hi - lo], T.wq[:], T.ws[:], T.bq[:, lo:hi], T.bs[:, lo:hi],
+                           True, True).then_inc(S["m%d" % k], 1)
+        on_vector = (len(banks) - 1 - k) % 2 == 0
+        q = g.vector if on_vector else g.scalar
+        q.wait_ge(S["m%d" % k], 1)
+        for c, y, m in pieces:
+            if m == 0:
+                continue
+            if on_vector:
+                q.tensor_copy(T.yo[:, y:y + m], ps[:, c:c + m]).then_inc(S.cv, 1)
+                done["cv"] += 1
+            else:
+                q.activation(T.yo[:, y:y + m], ps[:, c:c + m], ActivationFunctionType.Copy).then_inc(S.cs, 1)
+                done["cs"] += 1
+
+    for name, k in done.items():
+        if k:
+            g.sync.wait_ge(S[name], k)
+    g.sync.dma_start(T.y[:], T.yo[:]).then_inc(S.st, 16)
+    g.sync.wait_ge(S.st, 16)
+    g.wait_ge(S.sent, sent)

@@ -2,7 +2,6 @@ from concourse.mybir import dt, ActivationFunctionType
 
 NCOL = 256
 HALF = 128
-NBANK = 4
 KEEP = 2
 HELP = 4
 
@@ -22,8 +21,12 @@ SCRATCH = {
 SEMAPHORES = ["ld1", "ld2", "ldw", "q1", "q2", "qw", "fs", "fc", "a1", "a2", "a3",
               "m0", "m1", "m2", "m3", "cv", "cs", "st", "sent"]
 
+_KEPT = {}
+
 
 def _plan(cores, cnt, topo):
+    if "plan" in _KEPT:
+        return _KEPT["plan"]
     n = len(cores)
     every = range(topo.CORES_PER_CHIP * topo.CHIPS)
     win = []
@@ -38,19 +41,55 @@ def _plan(cores, cnt, topo):
     def wid(j, e):
         return win[j][e][1] - win[j][e][0]
 
-    via = []
+    def ports(h, c):
+        a, b, d = topo.chip(h), topo.chip(c), topo.die(h)
+        if topo.same_plane(a, b):
+            return [("out", a, d), ("in", b, d)]
+        if topo.mates(a, b):
+            return [("mate", a, d)]
+        m = [x for x in range(topo.CHIPS) if topo.mates(a, x)][0]
+        return [("mate", a, d), ("out", m, d), ("in", b, d)]
+
+    choices = []
     for j in range(n):
         me = cores[j]
         mine = [c for c in every if topo.chip(c) == topo.chip(me) and c not in cores]
-        mine.sort(key=lambda c: topo.die(c) == topo.die(me))
         far = sorted([e for e in win[j] if not topo.may_write(me, cores[e])], key=lambda e: -wid(j, e))
-        ports = [c for c in mine if all(topo.may_write(c, cores[e]) for e in far)]
-        v = {e: ports[i] for i, e in enumerate(far)}
-        near = sorted([e for e in win[j] if e not in v], key=lambda e: -wid(j, e))
-        free = [c for c in mine if c not in v.values()]
-        while len(near) > KEEP and len(v) < HELP:
-            v[near.pop()] = free.pop(0)
-        via.append(v)
+        near = sorted([e for e in win[j] if e not in far], key=lambda e: -wid(j, e))
+        passed = list(far)
+        while len(near) > KEEP and len(passed) < HELP:
+            passed.append(near.pop())
+        owner = [c for c in mine if all(topo.may_write(c, cores[e]) for e in far)]
+        dies = sorted(set(topo.die(c) for c in mine), key=lambda d: d == topo.die(me))
+        ways = []
+        for code in range(len(dies) ** len(passed)):
+            free, v = list(mine), {}
+            for e in passed:
+                d, code = dies[code % len(dies)], code // len(dies)
+                fit = [c for c in free if topo.die(c) == d and topo.may_write(c, cores[e])]
+                if e not in far:
+                    fit.sort(key=lambda c: c in owner)
+                if not fit:
+                    v = None
+                    break
+                v[e] = fit[0]
+                free.remove(fit[0])
+            if v is not None:
+                ways.append(v)
+        choices.append(ways)
+
+    def load(via):
+        on = {}
+        for j in range(n):
+            for e, h in via[j].items():
+                for p in ports(h, cores[e]):
+                    on[p] = on.get(p, 0) + wid(j, e)
+        return tuple(sorted(on.values(), reverse=True))
+
+    via = [ways[0] for ways in choices]
+    for _ in range(3):
+        for j in range(n):
+            via[j] = min(choices[j], key=lambda v: load(via[:j] + [v] + via[j + 1:]))
 
     base, groups = [], []
     for e in range(n):
@@ -59,19 +98,16 @@ def _plan(cores, cnt, topo):
         for j in order:
             b[j] = p
             p += wid(j, e)
-        gs, k = [], len(order)
-        while k > 0 and len(gs) < NBANK - 2:
-            i, s = k, 0
-            while i > 0 and s < HALF:
-                i -= 1
-                s += wid(order[i], e)
-            gs.insert(0, order[i:k])
-            k = i
-        if k > 0:
-            gs.insert(0, order[:k])
+        straight = [j for j in order if e not in via[j]]
+        late = [j for j in order if e in via[j]]
+        i, s = len(late), 0
+        while i > 0 and s < HALF:
+            i -= 1
+            s += wid(late[i], e)
         base.append(b)
-        groups.append(gs)
-    return win, via, base, groups
+        groups.append([grp for grp in (straight, late[:i], late[i:]) if grp])
+    _KEPT["plan"] = (win, via, base, groups)
+    return _KEPT["plan"]
 
 
 def _send(g, T, topo, src, dst, plane, a, b, at, sem):
@@ -118,7 +154,8 @@ def rank_program(g, core, T, topo):
         while left > 0:
             c = (turn + t) % NCOL
             m = min(left, NCOL - c)
-            g.sync.dma_start(T.xt[:, 4 * t:4 * (t + m)], T.x[:, 4 * c:4 * (c + m)]).then_inc(sem, 16)
+            q = g.scalar if k else g.sync
+            q.dma_start(T.xt[:, 4 * t:4 * (t + m)], T.x[:, 4 * c:4 * (c + m)]).then_inc(sem, 16)
             t, left, k = t + m, left - m, k + 1
         g.vector.wait_ge(sem, 16 * k)
         g.vector.quantize_mx(T.bq[:, h * HALF:(h + 1) * HALF], T.bs[:, h * HALF:(h + 1) * HALF],

from concourse.mybir import dt, ActivationFunctionType

NCOL = 256
HALF = 128
KEEP = 2
HELP = 4

SCRATCH = {
    "xt": ("sbuf", [128, 4 * NCOL], "bfloat16"),
    "wt": ("sbuf", [128, 512], "bfloat16"),
    "wq": ("sbuf", [128, 128], "float8_e4m3fn_x4"),
    "ws": ("sbuf", [128, 128], "uint8"),
    "bq": ("sbuf", [128, 3 * NCOL], "float8_e4m3fn_x4"),
    "bs": ("sbuf", [128, 3 * NCOL], "uint8"),
    "yo": ("sbuf", [128, 2 * NCOL], "float32"),
    "p0": ("psum", [128, 512], "float32"),
    "p1": ("psum", [128, 512], "float32"),
    "p2": ("psum", [128, 512], "float32"),
    "p3": ("psum", [128, 512], "float32"),
}
SEMAPHORES = ["ld1", "ld2", "ldw", "q1", "q2", "qw", "fs", "fc", "a1", "a2", "a3",
              "m0", "m1", "m2", "m3", "cv", "cs", "st", "sent"]

_KEPT = {}


def _plan(cores, cnt, topo):
    if "plan" in _KEPT:
        return _KEPT["plan"]
    n = len(cores)
    every = range(topo.CORES_PER_CHIP * topo.CHIPS)
    win = []
    for j in range(n):
        p, pos = 0, {}
        for i in range(n):
            pos[(j + i) % n] = p
            p += cnt[j][(j + i) % n]
        win.append({e: (pos[(e - 1) % n], pos[(e - 1) % n] + cnt[j][(e - 1) % n] + cnt[j][e])
                    for e in range(n) if e != j and cnt[j][(e - 1) % n] + cnt[j][e] > 0})

    def wid(j, e):
        return win[j][e][1] - win[j][e][0]

    def ports(h, c):
        a, b, d = topo.chip(h), topo.chip(c), topo.die(h)
        if topo.same_plane(a, b):
            return [("out", a, d), ("in", b, d)]
        if topo.mates(a, b):
            return [("mate", a, d)]
        m = [x for x in range(topo.CHIPS) if topo.mates(a, x)][0]
        return [("mate", a, d), ("out", m, d), ("in", b, d)]

    choices = []
    for j in range(n):
        me = cores[j]
        mine = [c for c in every if topo.chip(c) == topo.chip(me) and c not in cores]
        far = sorted([e for e in win[j] if not topo.may_write(me, cores[e])], key=lambda e: -wid(j, e))
        near = sorted([e for e in win[j] if e not in far], key=lambda e: -wid(j, e))
        passed = list(far)
        while len(near) > KEEP and len(passed) < HELP:
            passed.append(near.pop())
        owner = [c for c in mine if all(topo.may_write(c, cores[e]) for e in far)]
        dies = sorted(set(topo.die(c) for c in mine), key=lambda d: d == topo.die(me))
        ways = []
        for code in range(len(dies) ** len(passed)):
            free, v = list(mine), {}
            for e in passed:
                d, code = dies[code % len(dies)], code // len(dies)
                fit = [c for c in free if topo.die(c) == d and topo.may_write(c, cores[e])]
                if e not in far:
                    fit.sort(key=lambda c: c in owner)
                if not fit:
                    v = None
                    break
                v[e] = fit[0]
                free.remove(fit[0])
            if v is not None:
                ways.append(v)
        choices.append(ways)

    def load(via):
        on = {}
        for j in range(n):
            for e, h in via[j].items():
                for p in ports(h, cores[e]):
                    on[p] = on.get(p, 0) + wid(j, e)
        return tuple(sorted(on.values(), reverse=True))

    via = [ways[0] for ways in choices]
    for _ in range(3):
        for j in range(n):
            via[j] = min(choices[j], key=lambda v: load(via[:j] + [v] + via[j + 1:]))

    base, groups = [], []
    for e in range(n):
        order = sorted([j for j in range(n) if e in win[j]], key=lambda j: (e in via[j], wid(j, e), j))
        p, b = NCOL, {}
        for j in order:
            b[j] = p
            p += wid(j, e)
        straight = [j for j in order if e not in via[j]]
        late = [j for j in order if e in via[j]]
        i, s = len(late), 0
        while i > 0 and s < HALF:
            i -= 1
            s += wid(late[i], e)
        base.append(b)
        groups.append([grp for grp in (straight, late[:i], late[i:]) if grp])
    _KEPT["plan"] = (win, via, base, groups)
    return _KEPT["plan"]


def _send(g, T, topo, src, dst, plane, a, b, at, sem):
    rid, pid, _ = topo.addr(dst)
    m = topo.mask(src, dst)
    if plane:
        g.remote_dma(T.bs[:, at:at + b - a], T.bs[:, a:b], sem, T.sem.sent, pid, rid, m)
    else:
        g.remote_dma(T.bq[:, at:at + b - a].bitcast(dt.uint8), T.bq[:, a:b].bitcast(dt.uint8),
                     sem, T.sem.sent, pid, rid, m)
    return bin(m).count("1")


def rank_program(g, core, T, topo):
    cores, cnt = list(T.cores), T.tables["CNT"]
    n = len(cores)
    win, via, base, groups = _plan(cores, cnt, topo)
    S = T.sem

    def gsem(e, j):
        for k, grp in enumerate(groups[e]):
            if j in grp:
                return S["a%d" % (k + 1)]

    rank = T.rank_of(core)
    if rank is None:
        for j in range(n):
            for e, h in via[j].items():
                if h != core:
                    continue
                a, b = win[j][e]
                fed = bin(topo.mask(cores[j], core)).count("1")
                g.wait_ge(S.fs, fed)
                out = _send(g, T, topo, core, cores[e], True, a, b, base[e][j], gsem(e, j))
                g.wait_ge(S.fc, fed)
                out += _send(g, T, topo, core, cores[e], False, a, b, base[e][j], gsem(e, j))
                g.wait_ge(S.sent, out)
        return

    j = e = rank
    turn = sum(cnt[j][:j])
    for h, sem in ((0, S.ld1), (1, S.ld2)):
        t, left, k = h * HALF, HALF, 0
        while left > 0:
            c = (turn + t) % NCOL
            m = min(left, NCOL - c)
            q = g.scalar if k else g.sync
            q.dma_start(T.xt[:, 4 * t:4 * (t + m)], T.x[:, 4 * c:4 * (c + m)]).then_inc(sem, 16)
            t, left, k = t + m, left - m, k + 1
        g.vector.wait_ge(sem, 16 * k)
        g.vector.quantize_mx(T.bq[:, h * HALF:(h + 1) * HALF], T.bs[:, h * HALF:(h + 1) * HALF],
                             T.xt[:, 4 * h * HALF:4 * (h + 1) * HALF]).then_inc(S.q2 if h else S.q1, 1)
    g.sync.dma_start(T.wt[:], T.w[:]).then_inc(S.ldw, 16)
    g.vector.wait_ge(S.ldw, 16)
    g.vector.quantize_mx(T.wq[:], T.ws[:], T.wt[:]).then_inc(S.qw, 1)

    both = [False]

    def ready(b):
        if b > HALF and not both[0]:
            g.wait_ge(S.q2, 1)
            both[0] = True

    def wid(d):
        return win[j][d][1] - win[j][d][0]

    sent = 0
    g.wait_ge(S.q1, 1)
    fed = sorted(via[j], key=lambda d: -wid(d))
    for d in sorted(fed, key=lambda d: win[j][d][1] > HALF):
        a, b = win[j][d]
        ready(b)
        sent += _send(g, T, topo, core, via[j][d], True, a, b, a, S.fs)
    for d in fed:
        a, b = win[j][d]
        ready(b)
        sent += _send(g, T, topo, core, via[j][d], False, a, b, a, S.fc)
    for d in sorted([d for d in win[j] if d not in via[j]], key=lambda d: -wid(d)):
        a, b = win[j][d]
        ready(b)
        sent += _send(g, T, topo, core, cores[d], True, a, b, base[d][j], gsem(d, j))
        sent += _send(g, T, topo, core, cores[d], False, a, b, base[d][j], gsem(d, j))

    def ycol(k, s):
        f = (e - k) % n
        return k * NCOL + sum(cnt[i][f] for i in range(s))

    banks = [(0, NCOL, [(0, ycol(0, e), cnt[e][e]),
                        (NCOL - cnt[e][(e - 1) % n], ycol(1, e), cnt[e][(e - 1) % n])], None, 0)]
    for k, grp in enumerate(groups[e]):
        hi = base[e][grp[-1]] + win[grp[-1]][e][1] - win[grp[-1]][e][0]
        lo = min(base[e][grp[0]], hi - HALF)
        pieces, due = [], 0
        for s in grp:
            c1 = cnt[s][(e - 1) % n]
            pieces.append((base[e][s] - lo, ycol(1, s), c1))
            pieces.append((base[e][s] + c1 - lo, ycol(0, s), cnt[s][e]))
            due += 2 * bin(topo.mask(via[s].get(e, cores[s]), core)).count("1")
        banks.append((lo, hi, pieces, S["a%d" % (k + 1)], due))

    g.tensor.wait_ge(S.qw, 1)
    g.tensor.wait_ge(S.q1, 1)
    g.tensor.wait_ge(S.q2, 1)
    done = {"cv": 0, "cs": 0}
    for k, (lo, hi, pieces, sem, due) in enumerate(banks):
        if sem is not None:
            g.tensor.wait_ge(sem, due)
        ps = T["p%d" % k]
        g.tensor.matmul_mx(ps[:, 0:hi - lo], T.wq[:], T.ws[:], T.bq[:, lo:hi], T.bs[:, lo:hi],
                           True, True).then_inc(S["m%d" % k], 1)
        on_vector = (len(banks) - 1 - k) % 2 == 0
        q = g.vector if on_vector else g.scalar
        q.wait_ge(S["m%d" % k], 1)
        for c, y, m in pieces:
            if m == 0:
                continue
            if on_vector:
                q.tensor_copy(T.yo[:, y:y + m], ps[:, c:c + m]).then_inc(S.cv, 1)
                done["cv"] += 1
            else:
                q.activation(T.yo[:, y:y + m], ps[:, c:c + m], ActivationFunctionType.Copy).then_inc(S.cs, 1)
                done["cs"] += 1

    for name, k in done.items():
        if k:
            g.sync.wait_ge(S[name], k)
    g.sync.dma_start(T.y[:], T.yo[:]).then_inc(S.st, 16)
    g.sync.wait_ge(S.st, 16)
    g.wait_ge(S.sent, sent)
